import numpy as np, ml_dtypes
CORES = [76,84,92,100,108,116,124]
N = 7
F = 256
def setup_inputs(rng):
    return {"a": rng.standard_normal((N, 128, 128), dtype=np.float32).astype(ml_dtypes.bfloat16), "w": rng.standard_normal((N, 128, F), dtype=np.float32).astype(ml_dtypes.bfloat16)}
def setup_inputs_big(rng):
    d = setup_inputs(rng)
    for k in ("a", "w"): d[k] = (d[k].astype(np.float32) * 1024.0).astype(d[k].dtype)
    return d
def setup_inputs_small(rng):
    d = setup_inputs(rng)
    for k in ("a", "w"): d[k] = (d[k].astype(np.float32) * (1 / 1024.0)).astype(d[k].dtype)
    return d
def setup_inputs_apart(rng):
    d = setup_inputs(rng)
    f = (10.0 ** rng.permutation(np.linspace(-1.5, 1.5, N))).astype(np.float32).reshape(N, 1, 1)
    for k in ("a", "w"): d[k] = (d[k].astype(np.float32) * f).astype(d[k].dtype)
    return d
def reference(a, w):
    A, W = a.astype(np.float64), w.astype(np.float64)
    p = np.stack([A[j].T @ W[j] for j in range(N)])
    return {"y": np.cumsum(p, axis=0).astype(ml_dtypes.bfloat16 if a.dtype != np.float64 else np.float64)}

@@ -1,0 +1,168 @@
+from concourse.bass import DstId, RemoteDMATransfer
+from concourse.mybir import AluOpType
+
+F = 256
+ENGINES_A_WRITE = 4
+
+SCRATCH = {
+    "a_sb": ("sbuf", [128, 128], "bfloat16"),
+    "w_sb": ("sbuf", [128, F], "bfloat16"),
+    "p_bf": ("sbuf", [128, F], "bfloat16"),
+    "in0": ("sbuf", [128, F], "bfloat16"),
+    "in1": ("sbuf", [128, F], "bfloat16"),
+    "in2": ("sbuf", [128, F], "bfloat16"),
+    "landA": ("sbuf", [128, F], "bfloat16"),
+    "landB": ("sbuf", [128, F], "bfloat16"),
+    "y_sb": ("sbuf", [128, F], "bfloat16"),
+    "acc": ("psum", [128, F], "float32"),
+    "acc2": ("psum", [128, F], "float32"),
+}
+SEMAPHORES = ["loaded", "mm", "cp", "sent", "arrH", "arrA", "arrB", "v1", "v2", "stored"]
+
+
+def _bits(m):
+    return [b for b in range(m.bit_length()) if (m >> b) & 1]
+
+
+def _assign_masks(topo, src, writes, n):
+    allowed = [topo.mask(src, w["to"]) for w in writes]
+    narrow = allowed[0]
+    for m in allowed:
+        narrow &= m
+    taken = 0
+    for i in sorted(range(len(writes)), key=lambda k: len(_bits(allowed[k]))):
+        free = _bits(allowed[i] & ~taken)
+        wide_only = [b for b in free if not (narrow >> b) & 1]
+        if len(wide_only) >= n:
+            pick = wide_only[:n]
+        elif len(free) >= 2 * n:
+            pick = free[::2][:n]
+        else:
+            pick = free[:n]
+        assert len(pick) == n
+        m = sum(1 << b for b in pick)
+        taken |= m
+        writes[i]["mask"] = m
+
+
+def _plan(T, topo):
+    cores = list(T.cores)
+    n = len(cores)
+    chip = [topo.chip(c) for c in cores]
+    classes = []
+    for r in range(n):
+        for cl in classes:
+            if topo.may_write(cores[cl[0]], cores[r]) and topo.may_write(cores[r], cores[cl[0]]):
+                cl.append(r)
+                break
+        else:
+            classes.append([r])
+    pairs = [(lo, hi) for lo in range(n) for hi in range(lo + 1, n) if topo.mates(chip[lo], chip[hi])]
+    sends = {}
+    got = {r: [] for r in range(n)}
+    busy = set(cores)
+    for lo, hi in pairs:
+        assert hi == lo + 1
+        for cl in classes:
+            terms = [j for j in cl if j <= lo]
+            if not terms:
+                continue
+            dests = [r for r in (lo, hi) if terms != [r]]
+            site = terms[0] if len(terms) == 1 else [r for r in (lo, hi) if r in cl][0]
+            helper = [c for c in range(topo.CHIPS * topo.CORES_PER_CHIP)
+                      if topo.chip(c) == chip[site] and c not in busy and topo.die(c) == topo.die(cores[site])
+                      and all(topo.may_write(c, cores[r]) for r in dests)][0]
+            busy.add(helper)
+            for i, j in enumerate(terms):
+                sends.setdefault(cores[j], []).append(
+                    {"to": helper, "srcs": ["p_bf"], "dst": "in%d" % i, "sem": "arrH"})
+            far = sum(1 for j in terms if chip[j] != topo.chip(helper))
+            for r in dests:
+                w = {"to": cores[r], "srcs": ["in%d" % i for i in range(len(terms))], "terms": terms}
+                sends.setdefault(helper, []).append(w)
+                got[r].append((far, chip[r] != topo.chip(helper), w))
+    own = {}
+    for r in range(n):
+        ws = [t[2] for t in sorted(got[r], key=lambda t: t[:2])]
+        assert len(ws) <= 2
+        for w, slot in zip(reversed(ws), ("B", "A")):
+            w["dst"] = "land" + slot
+            w["sem"] = "arr" + slot
+        got[r] = ws
+        held = [j for w in ws for j in w["terms"]]
+        own[r] = r not in held
+        assert sorted(held + ([r] if own[r] else [])) == list(range(r + 1))
+    for c in sends:
+        _assign_masks(topo, c, sends[c], ENGINES_A_WRITE)
+    return sends, got, own
+
+
+def _issue(g, T, topo, writes):
+    trs = []
+    for w in writes:
+        rid, pid, _ring = topo.addr(w["to"])
+        to = [DstId(rid=rid, pnc=pid)]
+        srcs = [T[s][:] for s in w["srcs"]]
+        if len(srcs) == 1:
+            trs.append(RemoteDMATransfer(dst_ids=to, dma_engine_mask=w["mask"], remote_sem=T.sem[w["sem"]],
+                                         src=srcs[0], dst=T[w["dst"]][:], alu_op=0))
+        else:
+            trs.append(RemoteDMATransfer(dst_ids=to, dma_engine_mask=w["mask"], remote_sem=T.sem[w["sem"]],
+                                         srcs=srcs, dsts=[T[w["dst"]][:]], alu_op=1))
+    g.remote_dma_fused(trs, local_sem=T.sem.sent)
+    return sum(len(_bits(w["mask"])) for w in writes)
+
+
+def rank_program(g, core, T, topo):
+    sends, got, own = _plan(T, topo)
+    mine = sends.get(core, [])
+    rank = T.rank_of(core)
+
+    if rank is None:
+        if not mine:
+            return
+        due = sum(len(_bits(w["mask"])) for ws in sends.values() for w in ws if w["to"] == core)
+        g.wait_ge(T.sem.arrH, due)
+        left = _issue(g, T, topo, mine)
+        g.wait_ge(T.sem.sent, left)
+        return
+
+    arrivals = got[rank]
+    g.sync.dma_start(T.a_sb[:], T.a[:]).then_inc(T.sem.loaded, 16)
+    g.scalar.dma_start(T.w_sb[:], T.w[:]).then_inc(T.sem.loaded, 16)
+    g.tensor.wait_ge(T.sem.loaded, 32)
+    g.tensor.matmul(T.acc[:], T.a_sb[:], T.w_sb[:], True, True).then_inc(T.sem.mm, 1)
+    g.vector.wait_ge(T.sem.mm, 1)
+
+    left = 0
+    if mine or not arrivals:
+        g.vector.tensor_copy(T.p_bf[:], T.acc[:]).then_inc(T.sem.cp, 1)
+    if mine:
+        g.wait_ge(T.sem.cp, 1)
+        left = _issue(g, T, topo, mine)
+
+    if not arrivals:
+        g.sync.wait_ge(T.sem.cp, 1)
+        g.sync.dma_start(T.y[:], T.p_bf[:]).then_inc(T.sem.stored, 16)
+    else:
+        part = T.acc
+        if len(arrivals) == 2:
+            w = arrivals[0]
+            g.vector.wait_ge(T.sem[w["sem"]], len(_bits(w["mask"])))
+            if own[rank]:
+                g.vector.tensor_tensor(T.acc2[:], T.acc[:], T[w["dst"]][:], AluOpType.add).then_inc(T.sem.v1, 1)
+            else:
+                g.vector.tensor_copy(T.acc2[:], T[w["dst"]][:]).then_inc(T.sem.v1, 1)
+            g.vector.wait_ge(T.sem.v1, 1)
+            part = T.acc2
+        else:
+            assert own[rank]
+        w = arrivals[-1]
+        g.vector.wait_ge(T.sem[w["sem"]], len(_bits(w["mask"])))
+        g.vector.tensor_tensor(T.y_sb[:], part[:], T[w["dst"]][:], AluOpType.add).then_inc(T.sem.v2, 1)
+        g.sync.wait_ge(T.sem.v2, 1)
+        g.sync.dma_start(T.y[:], T.y_sb[:]).then_inc(T.sem.stored, 16)
+
+    if left:
+        g.wait_ge(T.sem.sent, left)
+    g.sync.wait_ge(T.sem.stored, 16)

@@ -2,7 +2,8 @@ from concourse.bass import DstId, RemoteDMATransfer
 from concourse.mybir import AluOpType
 
 F = 256
-ENGINES_A_WRITE = 4
+RANK_ENGINES = 8
+HELPER_ENGINES = 8
 
 SCRATCH = {
     "a_sb": ("sbuf", [128, 128], "bfloat16"),
@@ -24,22 +25,28 @@ def _bits(m):
     return [b for b in range(m.bit_length()) if (m >> b) & 1]
 
 
-def _assign_masks(topo, src, writes, n):
+def _assign_masks(topo, src, writes, want):
     allowed = [topo.mask(src, w["to"]) for w in writes]
     narrow = allowed[0]
     for m in allowed:
         narrow &= m
+    tight = sum(1 for m in allowed if m == narrow)
     taken = 0
     for i in sorted(range(len(writes)), key=lambda k: len(_bits(allowed[k]))):
+        n = want
+        if allowed[i] == narrow:
+            while n * tight > len(_bits(narrow)):
+                n //= 2
         free = _bits(allowed[i] & ~taken)
         wide_only = [b for b in free if not (narrow >> b) & 1]
+        while len(free) < n:
+            n //= 2
         if len(wide_only) >= n:
             pick = wide_only[:n]
         elif len(free) >= 2 * n:
             pick = free[::2][:n]
         else:
             pick = free[:n]
-        assert len(pick) == n
         m = sum(1 << b for b in pick)
         taken |= m
         writes[i]["mask"] = m
@@ -93,7 +100,7 @@ def _plan(T, topo):
         own[r] = r not in held
         assert sorted(held + ([r] if own[r] else [])) == list(range(r + 1))
     for c in sends:
-        _assign_masks(topo, c, sends[c], ENGINES_A_WRITE)
+        _assign_masks(topo, c, sends[c], RANK_ENGINES if c in cores else HELPER_ENGINES)
     return sends, got, own
 
 

@@ -2,8 +2,7 @@ from concourse.bass import DstId, RemoteDMATransfer
 from concourse.mybir import AluOpType
 
 F = 256
-RANK_ENGINES = 8
-HELPER_ENGINES = 8
+FOLD_FAR = 2
 
 SCRATCH = {
     "a_sb": ("sbuf", [128, 128], "bfloat16"),
@@ -12,13 +11,15 @@ SCRATCH = {
     "in0": ("sbuf", [128, F], "bfloat16"),
     "in1": ("sbuf", [128, F], "bfloat16"),
     "in2": ("sbuf", [128, F], "bfloat16"),
-    "landA": ("sbuf", [128, F], "bfloat16"),
-    "landB": ("sbuf", [128, F], "bfloat16"),
+    "land0": ("sbuf", [128, F], "bfloat16"),
+    "land1": ("sbuf", [128, F], "bfloat16"),
+    "land2": ("sbuf", [128, F], "bfloat16"),
+    "land3": ("sbuf", [128, F], "bfloat16"),
     "y_sb": ("sbuf", [128, F], "bfloat16"),
     "acc": ("psum", [128, F], "float32"),
     "acc2": ("psum", [128, F], "float32"),
 }
-SEMAPHORES = ["loaded", "mm", "cp", "sent", "arrH", "arrA", "arrB", "v1", "v2", "stored"]
+SEMAPHORES = ["loaded", "mm", "cp", "sent", "arrH", "arr0", "arr1", "arr2", "arr3", "v1", "v2", "stored"]
 
 
 def _bits(m):
@@ -64,44 +65,74 @@ def _plan(T, topo):
                 break
         else:
             classes.append([r])
-    pairs = [(lo, hi) for lo in range(n) for hi in range(lo + 1, n) if topo.mates(chip[lo], chip[hi])]
-    sends = {}
-    got = {r: [] for r in range(n)}
+    pairs = [(a, b) for a in range(n) for b in range(a + 1, n) if topo.mates(chip[a], chip[b])]
+    lo, hi = pairs[-1]
+    assert hi == lo + 1 == n - 1
     busy = set(cores)
-    for lo, hi in pairs:
-        assert hi == lo + 1
-        for cl in classes:
-            terms = [j for j in cl if j <= lo]
-            if not terms:
-                continue
-            dests = [r for r in (lo, hi) if terms != [r]]
-            site = terms[0] if len(terms) == 1 else [r for r in (lo, hi) if r in cl][0]
-            helper = [c for c in range(topo.CHIPS * topo.CORES_PER_CHIP)
-                      if topo.chip(c) == chip[site] and c not in busy and topo.die(c) == topo.die(cores[site])
-                      and all(topo.may_write(c, cores[r]) for r in dests)][0]
-            busy.add(helper)
-            for i, j in enumerate(terms):
-                sends.setdefault(cores[j], []).append(
-                    {"to": helper, "srcs": ["p_bf"], "dst": "in%d" % i, "sem": "arrH"})
-            far = sum(1 for j in terms if chip[j] != topo.chip(helper))
-            for r in dests:
-                w = {"to": cores[r], "srcs": ["in%d" % i for i in range(len(terms))], "terms": terms}
-                sends.setdefault(helper, []).append(w)
-                got[r].append((far, chip[r] != topo.chip(helper), w))
+
+    def port_core(site, dests):
+        c = [c for c in range(topo.CHIPS * topo.CORES_PER_CHIP)
+             if topo.chip(c) == chip[site] and c not in busy and topo.die(c) == topo.die(cores[site])
+             and all(topo.may_write(c, cores[r]) for r in dests)][0]
+        busy.add(c)
+        return c
+
+    first = {j: [] for j in range(n)}
+    feeds = {j: [] for j in range(n)}
+    direct = {j: [] for j in range(n)}
+    calls = {}
+    got = {r: [] for r in range(n)}
+    todo = []
+    for cl in classes:
+        terms = [j for j in cl if j <= lo]
+        helper = port_core([r for r in (lo, hi) if r in cl][0], (lo, hi))
+        away = [j for j in terms if chip[j] != topo.chip(helper)]
+        for j in away[FOLD_FAR:]:
+            terms.remove(j)
+            todo += [(j, r, True) for r in (lo, hi)]
+        for i, j in enumerate(terms):
+            first[j].append({"to": helper, "srcs": ["p_bf"], "dst": "in%d" % i, "sem": "arrH"})
+        far = sum(1 for j in terms if chip[j] != topo.chip(helper))
+        ws = []
+        for r in (lo, hi):
+            w = {"to": cores[r], "srcs": ["in%d" % i for i in range(len(terms))], "terms": terms}
+            ws.append(w)
+            got[r].append((56 + far + (chip[r] != topo.chip(helper)), w))
+        calls[helper] = [(ws, 8)]
+    todo += [(j, r, False) for j in range(lo) for r in range(lo - 1, j, -1)]
+    base = {j: 16 if first[j] else 8 for j in range(n)}
+    for j, r, forced in todo:
+        if topo.may_write(cores[j], cores[r]) and not forced:
+            direct[j].append({"to": cores[r], "srcs": ["p_bf"], "terms": [j]})
+        else:
+            relay = port_core(j, (r,))
+            f = {"to": relay, "srcs": ["p_bf"], "dst": "in0", "sem": "arrH"}
+            early = not any(topo.chip(w["to"]) == chip[j] for w in first[j])
+            (first[j] if early else feeds[j]).append(f)
+            w = {"to": cores[r], "srcs": ["in0"], "terms": [j]}
+            calls[relay] = [([w], 8)]
+            got[r].append((base[j] + 8 * len(feeds[j]) + 40, w))
+    for j in range(n):
+        for k, w in enumerate(direct[j]):
+            got[cores.index(w["to"])].append((base[j] + 8 * len(feeds[j]) + 16 * (k + 1), w))
+        cs = ([(first[j], 2 * base[j] if base[j] == 8 else 8)] if first[j] else [])
+        cs += [([f], 16) for f in feeds[j]] + [([w], 8) for w in direct[j]]
+        if cs:
+            calls[cores[j]] = cs
     own = {}
     for r in range(n):
-        ws = [t[2] for t in sorted(got[r], key=lambda t: t[:2])]
-        assert len(ws) <= 2
-        for w, slot in zip(reversed(ws), ("B", "A")):
-            w["dst"] = "land" + slot
-            w["sem"] = "arr" + slot
+        ws = [t[1] for t in sorted(got[r], key=lambda t: t[0])]
+        for k, w in enumerate(ws):
+            w["dst"] = "land%d" % k
+            w["sem"] = "arr%d" % k
         got[r] = ws
         held = [j for w in ws for j in w["terms"]]
         own[r] = r not in held
         assert sorted(held + ([r] if own[r] else [])) == list(range(r + 1))
-    for c in sends:
-        _assign_masks(topo, c, sends[c], RANK_ENGINES if c in cores else HELPER_ENGINES)
-    return sends, got, own
+    for c in calls:
+        for ws, want in calls[c]:
+            _assign_masks(topo, c, ws, want)
+    return {c: [ws for ws, _want in calls[c]] for c in calls}, got, own
 
 
 def _issue(g, T, topo, writes):
@@ -121,16 +152,16 @@ def _issue(g, T, topo, writes):
 
 
 def rank_program(g, core, T, topo):
-    sends, got, own = _plan(T, topo)
-    mine = sends.get(core, [])
+    calls, got, own = _plan(T, topo)
+    mine = calls.get(core, [])
     rank = T.rank_of(core)
 
     if rank is None:
         if not mine:
             return
-        due = sum(len(_bits(w["mask"])) for ws in sends.values() for w in ws if w["to"] == core)
+        due = sum(len(_bits(w["mask"])) for cs in calls.values() for ws in cs for w in ws if w["to"] == core)
         g.wait_ge(T.sem.arrH, due)
-        left = _issue(g, T, topo, mine)
+        left = sum(_issue(g, T, topo, ws) for ws in mine)
         g.wait_ge(T.sem.sent, left)
         return
 
@@ -142,31 +173,40 @@ def rank_program(g, core, T, topo):
     g.vector.wait_ge(T.sem.mm, 1)
 
     left = 0
-    if mine or not arrivals:
+    rounded = bool(mine) or not arrivals
+    if rounded:
         g.vector.tensor_copy(T.p_bf[:], T.acc[:]).then_inc(T.sem.cp, 1)
     if mine:
         g.wait_ge(T.sem.cp, 1)
-        left = _issue(g, T, topo, mine)
+        left = sum(_issue(g, T, topo, ws) for ws in mine)
 
     if not arrivals:
         g.sync.wait_ge(T.sem.cp, 1)
         g.sync.dma_start(T.y[:], T.p_bf[:]).then_inc(T.sem.stored, 16)
     else:
-        part = T.acc
-        if len(arrivals) == 2:
-            w = arrivals[0]
+        if rounded:
+            g.vector.wait_ge(T.sem.cp, 1)
+        part, spare = T.acc, T.acc2
+        have = own[rank]
+        done = 0
+        for k, w in enumerate(arrivals):
+            final = k == len(arrivals) - 1
             g.vector.wait_ge(T.sem[w["sem"]], len(_bits(w["mask"])))
-            if own[rank]:
-                g.vector.tensor_tensor(T.acc2[:], T.acc[:], T[w["dst"]][:], AluOpType.add).then_inc(T.sem.v1, 1)
+            if done:
+                g.vector.wait_ge(T.sem.v1, done)
+            out = T.y_sb if final else spare
+            if have:
+                op = g.vector.tensor_tensor(out[:], part[:], T[w["dst"]][:], AluOpType.add)
             else:
-                g.vector.tensor_copy(T.acc2[:], T[w["dst"]][:]).then_inc(T.sem.v1, 1)
-            g.vector.wait_ge(T.sem.v1, 1)
-            part = T.acc2
-        else:
-            assert own[rank]
-        w = arrivals[-1]
-        g.vector.wait_ge(T.sem[w["sem"]], len(_bits(w["mask"])))
-        g.vector.tensor_tensor(T.y_sb[:], part[:], T[w["dst"]][:], AluOpType.add).then_inc(T.sem.v2, 1)
+                assert not final
+                op = g.vector.tensor_copy(out[:], T[w["dst"]][:])
+            if final:
+                op.then_inc(T.sem.v2, 1)
+            else:
+                op.then_inc(T.sem.v1, 1)
+                done += 1
+                part, spare = spare, part
+                have = True
         g.sync.wait_ge(T.sem.v2, 1)
         g.sync.dma_start(T.y[:], T.y_sb[:]).then_inc(T.sem.stored, 16)
 

@@ -1,25 +1,31 @@
 from concourse.bass import DstId, RemoteDMATransfer
 from concourse.mybir import AluOpType
 
+K = 128
 F = 256
+BANK = 512
 FOLD_FAR = 2
 
 SCRATCH = {
-    "a_sb": ("sbuf", [128, 128], "bfloat16"),
-    "w_sb": ("sbuf", [128, F], "bfloat16"),
+    "aw_sb": ("sbuf", [128, K + F], "bfloat16"),
     "p_bf": ("sbuf", [128, F], "bfloat16"),
+    "rin": ("sbuf", [128, K + F], "bfloat16"),
+    "rland": ("sbuf", [128, K + F], "bfloat16"),
     "in0": ("sbuf", [128, F], "bfloat16"),
     "in1": ("sbuf", [128, F], "bfloat16"),
-    "in2": ("sbuf", [128, F], "bfloat16"),
     "land0": ("sbuf", [128, F], "bfloat16"),
     "land1": ("sbuf", [128, F], "bfloat16"),
     "land2": ("sbuf", [128, F], "bfloat16"),
     "land3": ("sbuf", [128, F], "bfloat16"),
+    "s0": ("sbuf", [128, F], "float32"),
+    "s1": ("sbuf", [128, F], "float32"),
     "y_sb": ("sbuf", [128, F], "bfloat16"),
-    "acc": ("psum", [128, F], "float32"),
-    "acc2": ("psum", [128, F], "float32"),
+    "acc": ("psum", [128, BANK], "float32"),
+    "accy": ("psum", [128, BANK], "float32"),
+    "q0": ("psum", [128, BANK], "float32"),
+    "q1": ("psum", [128, BANK], "float32"),
 }
-SEMAPHORES = ["loaded", "mm", "cp", "sent", "arrH", "arr0", "arr1", "arr2", "arr3", "v1", "v2", "stored"]
+SEMAPHORES = ["loaded", "mm", "mmy", "cp", "sent", "arrH", "arrR", "arr0", "arr1", "arr2", "arr3", "v1", "v2", "stored"]
 
 
 def _bits(m):
@@ -28,9 +34,8 @@ def _bits(m):
 
 def _assign_masks(topo, src, writes, want):
     allowed = [topo.mask(src, w["to"]) for w in writes]
-    narrow = allowed[0]
-    for m in allowed:
-        narrow &= m
+    away = [c for c in range(topo.CHIPS * topo.CORES_PER_CHIP) if topo.chip(c) != topo.chip(src)][0]
+    narrow = topo.mask(src, away)
     tight = sum(1 for m in allowed if m == narrow)
     taken = 0
     for i in sorted(range(len(writes)), key=lambda k: len(_bits(allowed[k]))):
@@ -82,9 +87,11 @@ def _plan(T, topo):
     direct = {j: [] for j in range(n)}
     calls = {}
     got = {r: [] for r in range(n)}
+    rawin = {}
+    rawfeed = {}
     todo = []
     for cl in classes:
-        terms = [j for j in cl if j <= lo]
+        terms = [j for j in cl if j < lo]
         helper = port_core([r for r in (lo, hi) if r in cl][0], (lo, hi))
         away = [j for j in terms if chip[j] != topo.chip(helper)]
         for j in away[FOLD_FAR:]:
@@ -99,15 +106,23 @@ def _plan(T, topo):
             ws.append(w)
             got[r].append((56 + far + (chip[r] != topo.chip(helper)), w))
         calls[helper] = [(ws, 8)]
+    for j in range(n - 1):
+        relay = port_core(j, (j + 1,))
+        rawfeed[j] = {"to": relay, "srcs": ["aw_sb"], "dst": "rin", "sem": "arrH", "raw": True}
+        w = {"to": cores[j + 1], "srcs": ["rin"], "dst": "rland", "sem": "arrR"}
+        calls[relay] = [([w], 8)]
+        rawin[j + 1] = w
     todo += [(j, r, False) for j in range(lo) for r in range(lo - 1, j, -1)]
     base = {j: 16 if first[j] else 8 for j in range(n)}
     for j, r, forced in todo:
+        if r == j + 1:
+            continue
         if topo.may_write(cores[j], cores[r]) and not forced:
-            direct[j].append({"to": cores[r], "srcs": ["p_bf"], "terms": [j]})
+            direct[j].append({"to": cores[r], "srcs": ["p_bf"], "terms": [j], "direct": True})
         else:
             relay = port_core(j, (r,))
             f = {"to": relay, "srcs": ["p_bf"], "dst": "in0", "sem": "arrH"}
-            early = not any(topo.chip(w["to"]) == chip[j] for w in first[j])
+            early = not first[j]
             (first[j] if early else feeds[j]).append(f)
             w = {"to": cores[r], "srcs": ["in0"], "terms": [j]}
             calls[relay] = [([w], 8)]
@@ -115,24 +130,23 @@ def _plan(T, topo):
     for j in range(n):
         for k, w in enumerate(direct[j]):
             got[cores.index(w["to"])].append((base[j] + 8 * len(feeds[j]) + 16 * (k + 1), w))
-        cs = ([(first[j], 2 * base[j] if base[j] == 8 else 8)] if first[j] else [])
+        cs = [([rawfeed[j]], 8 if base[j] == 16 else 16)] if j in rawfeed else []
+        cs += ([(first[j], 2 * base[j] if base[j] == 8 else 8)] if first[j] else [])
         cs += [([f], 16) for f in feeds[j]] + [([w], 8) for w in direct[j]]
         if cs:
             calls[cores[j]] = cs
-    own = {}
     for r in range(n):
-        ws = [t[1] for t in sorted(got[r], key=lambda t: t[0])]
+        ws = [t[1] for t in sorted(got[r], key=lambda t: (not t[1].get("direct", False), t[0]))]
         for k, w in enumerate(ws):
             w["dst"] = "land%d" % k
             w["sem"] = "arr%d" % k
         got[r] = ws
-        held = [j for w in ws for j in w["terms"]]
-        own[r] = r not in held
-        assert sorted(held + ([r] if own[r] else [])) == list(range(r + 1))
+        held = [j for w in ws for j in w["terms"]] + [r] + ([r - 1] if r in rawin else [])
+        assert sorted(held) == list(range(r + 1))
     for c in calls:
         for ws, want in calls[c]:
             _assign_masks(topo, c, ws, want)
-    return {c: [ws for ws, _want in calls[c]] for c in calls}, got, own
+    return {c: [ws for ws, _want in calls[c]] for c in calls}, got, rawin
 
 
 def _issue(g, T, topo, writes):
@@ -152,7 +166,7 @@ def _issue(g, T, topo, writes):
 
 
 def rank_program(g, core, T, topo):
-    calls, got, own = _plan(T, topo)
+    calls, got, rawin = _plan(T, topo)
     mine = calls.get(core, [])
     rank = T.rank_of(core)
 
@@ -166,47 +180,88 @@ def rank_program(g, core, T, topo):
         return
 
     arrivals = got[rank]
-    g.sync.dma_start(T.a_sb[:], T.a[:]).then_inc(T.sem.loaded, 16)
-    g.scalar.dma_start(T.w_sb[:], T.w[:]).then_inc(T.sem.loaded, 16)
-    g.tensor.wait_ge(T.sem.loaded, 32)
-    g.tensor.matmul(T.acc[:], T.a_sb[:], T.w_sb[:], True, True).then_inc(T.sem.mm, 1)
-    g.vector.wait_ge(T.sem.mm, 1)
+    raws = [ws for ws in mine if ws[0].get("raw", False)]
+    rest = [ws for ws in mine if not ws[0].get("raw", False)]
+    neighbour = rawin.get(rank)
+    rounded = bool(rest) or neighbour is None
+
+    g.sync.dma_start(T.aw_sb[:, 0:K], T.a[:]).then_inc(T.sem.loaded, 16)
+    g.scalar.dma_start(T.aw_sb[:, K:K + F], T.w[:]).then_inc(T.sem.loaded, 16)
 
     left = 0
-    rounded = bool(mine) or not arrivals
-    if rounded:
-        g.vector.tensor_copy(T.p_bf[:], T.acc[:]).then_inc(T.sem.cp, 1)
-    if mine:
+    if raws:
+        g.wait_ge(T.sem.loaded, 32)
+        left += sum(_issue(g, T, topo, ws) for ws in raws)
+    if rest:
         g.wait_ge(T.sem.cp, 1)
-        left = sum(_issue(g, T, topo, ws) for ws in mine)
+        left += sum(_issue(g, T, topo, ws) for ws in rest)
 
-    if not arrivals:
+    g.tensor.wait_ge(T.sem.loaded, 32)
+    if rounded:
+        g.tensor.matmul(T.acc[:, 0:F], T.aw_sb[:, 0:K], T.aw_sb[:, K:K + F], True, True).then_inc(T.sem.mm, 1)
+    if neighbour is not None:
+        g.tensor.matmul(T.accy[:, 0:F], T.aw_sb[:, 0:K], T.aw_sb[:, K:K + F], True, False)
+        g.tensor.wait_ge(T.sem.arrR, len(_bits(neighbour["mask"])))
+        g.tensor.matmul(T.accy[:, 0:F], T.rland[:, 0:K], T.rland[:, K:K + F], False, True).then_inc(T.sem.mmy, 1)
+
+    if rounded:
+        g.vector.wait_ge(T.sem.mm, 1)
+        g.vector.tensor_copy(T.p_bf[:], T.acc[:, 0:F]).then_inc(T.sem.cp, 1)
+
+    if neighbour is None:
         g.sync.wait_ge(T.sem.cp, 1)
         g.sync.dma_start(T.y[:], T.p_bf[:]).then_inc(T.sem.stored, 16)
     else:
-        if rounded:
-            g.vector.wait_ge(T.sem.cp, 1)
-        part, spare = T.acc, T.acc2
-        have = own[rank]
+        early = [w for w in arrivals if w.get("direct", False)]
+        late = [w for w in arrivals if not w.get("direct", False)]
         done = 0
-        for k, w in enumerate(arrivals):
-            final = k == len(arrivals) - 1
+        s = None
+        sbufs = [T.s0, T.s1]
+        for w in early:
             g.vector.wait_ge(T.sem[w["sem"]], len(_bits(w["mask"])))
+            if s is None:
+                s = T[w["dst"]]
+                continue
             if done:
                 g.vector.wait_ge(T.sem.v1, done)
-            out = T.y_sb if final else spare
-            if have:
-                op = g.vector.tensor_tensor(out[:], part[:], T[w["dst"]][:], AluOpType.add)
+            out = sbufs[done % 2]
+            g.vector.tensor_tensor(out[:], s[:], T[w["dst"]][:], AluOpType.add).then_inc(T.sem.v1, 1)
+            done += 1
+            s = out
+        g.vector.wait_ge(T.sem.mmy, 1)
+        if done:
+            g.vector.wait_ge(T.sem.v1, done)
+        part = T.accy
+        spare = [T.q0, T.q1]
+        nq = 0
+        if s is not None or not late:
+            final = not late
+            out = T.y_sb[:] if final else spare[nq % 2][:, 0:F]
+            if s is not None:
+                op = g.vector.tensor_tensor(out, part[:, 0:F], s[:], AluOpType.add)
             else:
-                assert not final
-                op = g.vector.tensor_copy(out[:], T[w["dst"]][:])
+                op = g.vector.tensor_copy(out, part[:, 0:F])
             if final:
                 op.then_inc(T.sem.v2, 1)
             else:
                 op.then_inc(T.sem.v1, 1)
                 done += 1
-                part, spare = spare, part
-                have = True
+                part = spare[nq % 2]
+                nq += 1
+        for k, w in enumerate(late):
+            final = k == len(late) - 1
+            g.vector.wait_ge(T.sem[w["sem"]], len(_bits(w["mask"])))
+            if done:
+                g.vector.wait_ge(T.sem.v1, done)
+            out = T.y_sb[:] if final else spare[nq % 2][:, 0:F]
+            op = g.vector.tensor_tensor(out, part[:, 0:F], T[w["dst"]][:], AluOpType.add)
+            if final:
+                op.then_inc(T.sem.v2, 1)
+            else:
+                op.then_inc(T.sem.v1, 1)
+                done += 1
+                part = spare[nq % 2]
+                nq += 1
         g.sync.wait_ge(T.sem.v2, 1)
         g.sync.dma_start(T.y[:], T.y_sb[:]).then_inc(T.sem.stored, 16)
 

from concourse.bass import DstId, RemoteDMATransfer
from concourse.mybir import AluOpType

K = 128
F = 256
BANK = 512
FOLD_FAR = 2

SCRATCH = {
    "aw_sb": ("sbuf", [128, K + F], "bfloat16"),
    "p_bf": ("sbuf", [128, F], "bfloat16"),
    "rin": ("sbuf", [128, K + F], "bfloat16"),
    "rland": ("sbuf", [128, K + F], "bfloat16"),
    "in0": ("sbuf", [128, F], "bfloat16"),
    "in1": ("sbuf", [128, F], "bfloat16"),
    "land0": ("sbuf", [128, F], "bfloat16"),
    "land1": ("sbuf", [128, F], "bfloat16"),
    "land2": ("sbuf", [128, F], "bfloat16"),
    "land3": ("sbuf", [128, F], "bfloat16"),
    "s0": ("sbuf", [128, F], "float32"),
    "s1": ("sbuf", [128, F], "float32"),
    "y_sb": ("sbuf", [128, F], "bfloat16"),
    "acc": ("psum", [128, BANK], "float32"),
    "accy": ("psum", [128, BANK], "float32"),
    "q0": ("psum", [128, BANK], "float32"),
    "q1": ("psum", [128, BANK], "float32"),
}
SEMAPHORES = ["loaded", "mm", "mmy", "cp", "sent", "arrH", "arrR", "arr0", "arr1", "arr2", "arr3", "v1", "v2", "stored"]


def _bits(m):
    return [b for b in range(m.bit_length()) if (m >> b) & 1]


def _assign_masks(topo, src, writes, want):
    allowed = [topo.mask(src, w["to"]) for w in writes]
    away = [c for c in range(topo.CHIPS * topo.CORES_PER_CHIP) if topo.chip(c) != topo.chip(src)][0]
    narrow = topo.mask(src, away)
    tight = sum(1 for m in allowed if m == narrow)
    taken = 0
    for i in sorted(range(len(writes)), key=lambda k: len(_bits(allowed[k]))):
        n = want
        if allowed[i] == narrow:
            while n * tight > len(_bits(narrow)):
                n //= 2
        free = _bits(allowed[i] & ~taken)
        wide_only = [b for b in free if not (narrow >> b) & 1]
        while len(free) < n:
            n //= 2
        if len(wide_only) >= n:
            pick = wide_only[:n]
        elif len(free) >= 2 * n:
            pick = free[::2][:n]
        else:
            pick = free[:n]
        m = sum(1 << b for b in pick)
        taken |= m
        writes[i]["mask"] = m


def _plan(T, topo):
    cores = list(T.cores)
    n = len(cores)
    chip = [topo.chip(c) for c in cores]
    classes = []
    for r in range(n):
        for cl in classes:
            if topo.may_write(cores[cl[0]], cores[r]) and topo.may_write(cores[r], cores[cl[0]]):
                cl.append(r)
                break
        else:
            classes.append([r])
    pairs = [(a, b) for a in range(n) for b in range(a + 1, n) if topo.mates(chip[a], chip[b])]
    lo, hi = pairs[-1]
    assert hi == lo + 1 == n - 1
    busy = set(cores)

    def port_core(site, dests):
        c = [c for c in range(topo.CHIPS * topo.CORES_PER_CHIP)
             if topo.chip(c) == chip[site] and c not in busy and topo.die(c) == topo.die(cores[site])
             and all(topo.may_write(c, cores[r]) for r in dests)][0]
        busy.add(c)
        return c

    first = {j: [] for j in range(n)}
    feeds = {j: [] for j in range(n)}
    direct = {j: [] for j in range(n)}
    calls = {}
    got = {r: [] for r in range(n)}
    rawin = {}
    rawfeed = {}
    todo = []
    for cl in classes:
        terms = [j for j in cl if j < lo]
        helper = port_core([r for r in (lo, hi) if r in cl][0], (lo, hi))
        away = [j for j in terms if chip[j] != topo.chip(helper)]
        for j in away[FOLD_FAR:]:
            terms.remove(j)
            todo += [(j, r, True) for r in (lo, hi)]
        for i, j in enumerate(terms):
            first[j].append({"to": helper, "srcs": ["p_bf"], "dst": "in%d" % i, "sem": "arrH"})
        far = sum(1 for j in terms if chip[j] != topo.chip(helper))
        ws = []
        for r in (lo, hi):
            w = {"to": cores[r], "srcs": ["in%d" % i for i in range(len(terms))], "terms": terms}
            ws.append(w)
            got[r].append((56 + far + (chip[r] != topo.chip(helper)), w))
        calls[helper] = [(ws, 8)]
    for j in range(n - 1):
        relay = port_core(j, (j + 1,))
        rawfeed[j] = {"to": relay, "srcs": ["aw_sb"], "dst": "rin", "sem": "arrH", "raw": True}
        w = {"to": cores[j + 1], "srcs": ["rin"], "dst": "rland", "sem": "arrR"}
        calls[relay] = [([w], 8)]
        rawin[j + 1] = w
    todo += [(j, r, False) for j in range(lo) for r in range(lo - 1, j, -1)]
    base = {j: 16 if first[j] else 8 for j in range(n)}
    for j, r, forced in todo:
        if r == j + 1:
            continue
        if topo.may_write(cores[j], cores[r]) and not forced:
            direct[j].append({"to": cores[r], "srcs": ["p_bf"], "terms": [j], "direct": True})
        else:
            relay = port_core(j, (r,))
            f = {"to": relay, "srcs": ["p_bf"], "dst": "in0", "sem": "arrH"}
            early = not first[j]
            (first[j] if early else feeds[j]).append(f)
            w = {"to": cores[r], "srcs": ["in0"], "terms": [j]}
            calls[relay] = [([w], 8)]
            got[r].append((base[j] + 8 * len(feeds[j]) + 40, w))
    for j in range(n):
        for k, w in enumerate(direct[j]):
            got[cores.index(w["to"])].append((base[j] + 8 * len(feeds[j]) + 16 * (k + 1), w))
        cs = [([rawfeed[j]], 8 if base[j] == 16 else 16)] if j in rawfeed else []
        cs += ([(first[j], 2 * base[j] if base[j] == 8 else 8)] if first[j] else [])
        cs += [([f], 16) for f in feeds[j]] + [([w], 8) for w in direct[j]]
        if cs:
            calls[cores[j]] = cs
    for r in range(n):
        ws = [t[1] for t in sorted(got[r], key=lambda t: (not t[1].get("direct", False), t[0]))]
        for k, w in enumerate(ws):
            w["dst"] = "land%d" % k
            w["sem"] = "arr%d" % k
        got[r] = ws
        held = [j for w in ws for j in w["terms"]] + [r] + ([r - 1] if r in rawin else [])
        assert sorted(held) == list(range(r + 1))
    for c in calls:
        for ws, want in calls[c]:
            _assign_masks(topo, c, ws, want)
    return {c: [ws for ws, _want in calls[c]] for c in calls}, got, rawin


def _issue(g, T, topo, writes):
    trs = []
    for w in writes:
        rid, pid, _ring = topo.addr(w["to"])
        to = [DstId(rid=rid, pnc=pid)]
        srcs = [T[s][:] for s in w["srcs"]]
        if len(srcs) == 1:
            trs.append(RemoteDMATransfer(dst_ids=to, dma_engine_mask=w["mask"], remote_sem=T.sem[w["sem"]],
                                         src=srcs[0], dst=T[w["dst"]][:], alu_op=0))
        else:
            trs.append(RemoteDMATransfer(dst_ids=to, dma_engine_mask=w["mask"], remote_sem=T.sem[w["sem"]],
                                         srcs=srcs, dsts=[T[w["dst"]][:]], alu_op=1))
    g.remote_dma_fused(trs, local_sem=T.sem.sent)
    return sum(len(_bits(w["mask"])) for w in writes)


def rank_program(g, core, T, topo):
    calls, got, rawin = _plan(T, topo)
    mine = calls.get(core, [])
    rank = T.rank_of(core)

    if rank is None:
        if not mine:
            return
        due = sum(len(_bits(w["mask"])) for cs in calls.values() for ws in cs for w in ws if w["to"] == core)
        g.wait_ge(T.sem.arrH, due)
        left = sum(_issue(g, T, topo, ws) for ws in mine)
        g.wait_ge(T.sem.sent, left)
        return

    arrivals = got[rank]
    raws = [ws for ws in mine if ws[0].get("raw", False)]
    rest = [ws for ws in mine if not ws[0].get("raw", False)]
    neighbour = rawin.get(rank)
    rounded = bool(rest) or neighbour is None

    g.sync.dma_start(T.aw_sb[:, 0:K], T.a[:]).then_inc(T.sem.loaded, 16)
    g.scalar.dma_start(T.aw_sb[:, K:K + F], T.w[:]).then_inc(T.sem.loaded, 16)

    left = 0
    if raws:
        g.wait_ge(T.sem.loaded, 32)
        left += sum(_issue(g, T, topo, ws) for ws in raws)
    if rest:
        g.wait_ge(T.sem.cp, 1)
        left += sum(_issue(g, T, topo, ws) for ws in rest)

    g.tensor.wait_ge(T.sem.loaded, 32)
    if rounded:
        g.tensor.matmul(T.acc[:, 0:F], T.aw_sb[:, 0:K], T.aw_sb[:, K:K + F], True, True).then_inc(T.sem.mm, 1)
    if neighbour is not None:
        g.tensor.matmul(T.accy[:, 0:F], T.aw_sb[:, 0:K], T.aw_sb[:, K:K + F], True, False)
        g.tensor.wait_ge(T.sem.arrR, len(_bits(neighbour["mask"])))
        g.tensor.matmul(T.accy[:, 0:F], T.rland[:, 0:K], T.rland[:, K:K + F], False, True).then_inc(T.sem.mmy, 1)

    if rounded:
        g.vector.wait_ge(T.sem.mm, 1)
        g.vector.tensor_copy(T.p_bf[:], T.acc[:, 0:F]).then_inc(T.sem.cp, 1)

    if neighbour is None:
        g.sync.wait_ge(T.sem.cp, 1)
        g.sync.dma_start(T.y[:], T.p_bf[:]).then_inc(T.sem.stored, 16)
    else:
        early = [w for w in arrivals if w.get("direct", False)]
        late = [w for w in arrivals if not w.get("direct", False)]
        done = 0
        s = None
        sbufs = [T.s0, T.s1]
        for w in early:
            g.vector.wait_ge(T.sem[w["sem"]], len(_bits(w["mask"])))
            if s is None:
                s = T[w["dst"]]
                continue
            if done:
                g.vector.wait_ge(T.sem.v1, done)
            out = sbufs[done % 2]
            g.vector.tensor_tensor(out[:], s[:], T[w["dst"]][:], AluOpType.add).then_inc(T.sem.v1, 1)
            done += 1
            s = out
        g.vector.wait_ge(T.sem.mmy, 1)
        if done:
            g.vector.wait_ge(T.sem.v1, done)
        part = T.accy
        spare = [T.q0, T.q1]
        nq = 0
        if s is not None or not late:
            final = not late
            out = T.y_sb[:] if final else spare[nq % 2][:, 0:F]
            if s is not None:
                op = g.vector.tensor_tensor(out, part[:, 0:F], s[:], AluOpType.add)
            else:
                op = g.vector.tensor_copy(out, part[:, 0:F])
            if final:
                op.then_inc(T.sem.v2, 1)
            else:
                op.then_inc(T.sem.v1, 1)
                done += 1
                part = spare[nq % 2]
                nq += 1
        for k, w in enumerate(late):
            final = k == len(late) - 1
            g.vector.wait_ge(T.sem[w["sem"]], len(_bits(w["mask"])))
            if done:
                g.vector.wait_ge(T.sem.v1, done)
            out = T.y_sb[:] if final else spare[nq % 2][:, 0:F]
            op = g.vector.tensor_tensor(out, part[:, 0:F], T[w["dst"]][:], AluOpType.add)
            if final:
                op.then_inc(T.sem.v2, 1)
            else:
                op.then_inc(T.sem.v1, 1)
                done += 1
                part = spare[nq % 2]
                nq += 1
        g.sync.wait_ge(T.sem.v2, 1)
        g.sync.dma_start(T.y[:], T.y_sb[:]).then_inc(T.sem.stored, 16)

    if left:
        g.wait_ge(T.sem.sent, left)
    g.sync.wait_ge(T.sem.stored, 16)
